import numpy as np
import ml_dtypes


def mxq(x, axis, fmt="e4m3"):
    dtype, down = {"e4m3": (ml_dtypes.float8_e4m3fn, 7), "e5m2": (ml_dtypes.float8_e5m2, 14)}[fmt]
    v = np.moveaxis(np.asarray(x, np.float32).astype(ml_dtypes.bfloat16).astype(np.float64), axis, -1)
    blocks = v.reshape(v.shape[:-1] + (-1, 32))
    amax = np.abs(blocks).max(-1, keepdims=True)
    byte = np.maximum(np.where(amax > 0, np.frexp(amax)[1] - 1 + 127, 0) - down, 1)
    scale = np.exp2(byte - 127.0)
    codes = (blocks / scale).astype(np.float32).astype(dtype).astype(np.float64)
    return np.moveaxis((codes * scale).reshape(v.shape), -1, axis)


WIDE = False


def mx_kscale(k):
    if not WIDE:
        return np.ones(k)
    levels = np.array([10, -10, 5, -5, 0])
    if k % 512:
        return np.exp2(np.random.permutation(np.resize(levels, k // 32))).repeat(32)
    a = np.empty((k // 512, 16))
    for p in range(k // 512):
        a[p, :8] = np.random.permutation(np.resize(levels, 8))
        for g in range(8):
            far = levels[np.abs(levels - a[p, g]) >= 10]
            a[p, g + 8] = far[np.random.randint(len(far))]
    return np.exp2(a.ravel()).repeat(32)


def f64(x):
    return np.asarray(x).astype(np.float64)


def striped(idx):
    return np.tile(np.asarray(idx).reshape(-1, 16).T, (8, 1)).astype(np.uint16)


def unstriped(offs):
    return offs[:16].T.reshape(-1).astype(np.int64)


E2M1 = np.array([0.0, 0.5, 1.0, 1.5, 2.0, 3.0, 4.0, 6.0, -0.0, -0.5, -1.0, -1.5, -2.0, -3.0, -4.0, -6.0])


def pack_weight(w, fmt):
    k, n = w.shape
    w = f64(np.asarray(w, np.float32).astype(ml_dtypes.bfloat16)).reshape(k // 32, 32, n)
    amax = np.abs(w).max(1)
    if fmt == "e4m3":
        byte = np.frexp(amax)[1] - 1 + 127 - 7
    else:
        mant, ex = np.frexp(amax / 6.0)
        byte = np.where(mant > 0.5, ex, ex - 1) + 127
    byte = np.clip(np.where(amax > 0, byte, 1), 1, 254)
    scaled = (w * np.exp2(127.0 - byte)[:, None, :]).reshape(k, n).astype(np.float32)
    by_word = np.ascontiguousarray(scaled.reshape(k // 512, 128, 4, n).transpose(0, 1, 3, 2))
    if fmt == "e4m3":
        words = by_word.astype(ml_dtypes.float8_e4m3fn).view(np.uint8)
    else:
        c = by_word.astype(ml_dtypes.float4_e2m1fn).view(np.uint8) & 0xF
        words = (c[..., 0::2] | (c[..., 1::2] << 4)).reshape(k // 512, 128, 2 * n)
    return np.ascontiguousarray(words), np.ascontiguousarray(byte.astype(np.uint8).reshape(k // 512, 16, n))


def unpack_weight(words, scales, fmt):
    g, _, n = scales.shape
    words = np.ascontiguousarray(words).reshape(g, 128, n, -1)
    if fmt == "e4m3":
        vals = words.view(ml_dtypes.float8_e4m3fn).astype(np.float64)
    else:
        nib = np.empty((g, 128, n, 4), np.uint8)
        nib[..., 0::2] = words & 0xF
        nib[..., 1::2] = words >> 4
        vals = E2M1[nib]
    vals = vals * np.repeat(np.exp2(scales.astype(np.float64) - 127.0), 8, axis=1)[..., None]
    return vals.transpose(0, 1, 3, 2).reshape(g * 512, n)


def sigmoid(v):
    return 1.0 / (1.0 + np.exp(-v))


D, T, I, Q, E, U, J, K = 512, 1024, 512, 256, 512, 1024, 512, 512


def setup_inputs():
    n = np.random.standard_normal
    idx = np.random.permutation(T)[:I]
    idx2 = np.random.permutation(U)[:J]
    fd = mx_kscale(D)
    fi = mx_kscale(I)
    fj = mx_kscale(J)
    fk = mx_kscale(K)
    ti = np.ones(T)
    ti[idx] = fi
    tj = np.ones(U)
    tj[idx2] = fj
    keysp = pack_weight(n((D, T)) / fd[:, None], "e2m1")
    ikeyp = pack_weight(n((D, U)) / fd[:, None], "e4m3")
    return {
        "query": (n((D, Q)) * 0.25 / np.sqrt(D) * fd[:, None]).astype(np.float32),
        "query2": (n((D, Q)) * 0.25 / np.sqrt(D) * fd[:, None]).astype(np.float32),
        "keys_words": keysp[0],
        "keys_scales": keysp[1],
        "ikey_words": ikeyp[0],
        "ikey_scales": ikeyp[1],
        "size": (np.random.uniform(4.0, 12.0, (1, I)) * fi).astype(np.float32),
        "isz": (np.random.uniform(4.0, 12.0, (1, J)) * fj).astype(np.float32),
        "vals": (n((E, T)) / ti).astype(np.float32),
        "ival": (n((E, U)) / tj).astype(np.float32),
        "inp": (n((K, Q)) * fk[:, None]).astype(np.float32),
        "wg": (n((K, E)) * 1 / np.sqrt(K) / fk[:, None]).astype(np.float32),
        "offs": striped(idx),
        "offs2": striped(idx2),
    }


def reference(query, query2, keys_words, keys_scales, ikey_words, ikey_scales, size, isz, vals, ival, inp, wg, offs, offs2):
    idx = unstriped(offs)
    idx2 = unstriped(offs2)
    keysu = unpack_weight(keys_words, keys_scales, "e2m1")
    ikeyu = unpack_weight(ikey_words, ikey_scales, "e4m3")
    queryq = mxq(f64(query), 0, "e4m3")
    keysidxg = keysu[:, idx]
    a = queryq.T @ keysidxg
    query2q = mxq(f64(query2), 0, "e4m3")
    ikeyidx2g = ikeyu[:, idx2]
    b = query2q.T @ ikeyidx2g
    p = np.exp(a - np.max(a, axis=1, keepdims=True))
    w = p * f64(size) / np.sum(p, axis=1, keepdims=True)
    wt = w.T
    px = np.exp(b - np.max(b, axis=1, keepdims=True))
    wx = px * f64(isz) / np.sum(px, axis=1, keepdims=True)
    wtx = wx.T
    vt = f64(vals)[:, idx].T
    ut = f64(ival)[:, idx2].T
    vtq = mxq(vt, 0, "e4m3")
    wtq = mxq(wt, 0, "e4m3")
    o = vtq.T @ wtq
    utq = mxq(ut, 0, "e4m3")
    wtxq = mxq(wtx, 0, "e4m3")
    ob = utq.T @ wtxq
    wgq = mxq(f64(wg), 0, "e4m3")
    inpq = mxq(f64(inp), 0, "e4m3")
    z = wgq.T @ inpq
    g = sigmoid(z)
    y = g * o + (1.0 - g) * ob
    return y

@@ -1,0 +1,249 @@
+from contextlib import ExitStack
+
+import concourse.mybir as mybir
+from concourse.masks import make_identity
+
+F32 = mybir.dt.float32
+BF16 = mybir.dt.bfloat16
+I32 = mybir.dt.int32
+U32 = mybir.dt.uint32
+U16 = mybir.dt.uint16
+U8 = mybir.dt.uint8
+FP8X4 = mybir.dt.float8_e4m3fn_x4
+FP4X4 = mybir.dt.float4_e2m1fn_x4
+ALU = mybir.AluOpType
+ACT = mybir.ActivationFunctionType
+AXIS = mybir.AxisListType
+
+P = 128
+POOL = 1024
+SLOTS = 512
+ROWS = 256
+FEATS = 512
+FLOPS = 5 * 2 * 512 * 512 * 256
+
+
+def tile_attend_fusegate_kernel(tc, query, query2, keys_words, keys_scales, ikey_words, ikey_scales,
+                                 size, isz, vals, ival, inp, wg, offs, offs2, out):
+    nc = tc.nc
+    with ExitStack() as ctx:
+        sb = ctx.enter_context(tc.tile_pool(name="sb", bufs=1))
+        ps = ctx.enter_context(tc.psum_pool(name="ps", bufs=1))
+
+        def sbt(name, shape, dtype, tag=None):
+            return sb.tile(shape, dtype, name=name, tag=tag or name, align_bytes=64)
+
+        def bank(name, tag, shape):
+            return ps.tile(shape, F32, name=name, tag=tag)
+
+        lists = [sbt("list0", [P, SLOTS // 16], U16), sbt("list1", [P, SLOTS // 16], U16)]
+        kwin = [sbt("kwin0", [P, POOL], U16), sbt("kwin1", [P, POOL], U32)]
+        swin = [sbt("swin0", [P, POOL], U8), sbt("swin1", [P, POOL], U8)]
+        qraw = [sbt("qraw%d" % a, [P, 4, ROWS], F32) for a in range(2)]
+        wcol = [sbt("wcol%d" % a, [P, 4], F32) for a in range(2)]
+        vwin = [[sbt("vwin%d_%d" % (a, b), [P, POOL], F32) for b in range(4)] for a in range(2)]
+        inraw = sbt("inraw", [P, 4, ROWS], F32)
+        wgraw = sbt("wgraw", [P, 4, FEATS], F32)
+        ident = sbt("ident", [P, P], F32)
+
+        def load_scales(a, src, quads):
+            for q in quads:
+                nc.sync.dma_start(out=swin[a][32 * q:32 * q + 4, :].bitcast(I32), in_=src[0, 4 * q:4 * q + 4, :].bitcast(I32))
+
+        def load_rows(dst, src):
+            nc.sync.dma_start(out=dst[:], in_=src.rearrange("(p t) w -> p t w", t=4))
+
+        def load_vals(a, b):
+            nc.sync.dma_start(out=vwin[a][b][:], in_=(vals, ival)[a][b * P:(b + 1) * P, :])
+
+
+        def quantise(name, src, width, tag=None):
+            codes = sbt(name + "_c", [P, width], U32, tag)
+            scales = sbt(name + "_s", [P, width], U8)
+            nc.vector.quantize_mx(out=codes[:].bitcast(FP8X4), scales=scales[:], in_=src[:])
+            return codes, scales
+
+        def weave(name, raw, width, on_vector=False, tag=None):
+            woven = sbt(name + "_b", [P, 4 * width], BF16, tag)
+            dst = woven[:].rearrange("p (c i t) -> p c t i", i=4, t=4)
+            src = raw.rearrange("p t (c i) -> p c t i", i=4)
+            if on_vector:
+                nc.vector.tensor_copy(out=dst, in_=src)
+            else:
+                nc.scalar.activation(out=dst, in_=src, func=ACT.Copy)
+            return woven
+
+        def gather_words(a):
+            kw = sbt("kw%d" % a, [P, SLOTS], (U16, U32)[a])
+            nc.vector.tensor_copy(kw[:], kwin[a][:].indirect(lists[a][:]))
+            return kw
+
+        def gather_scales(a):
+            ks = sbt("ks%d" % a, [P, SLOTS], U8)
+            nc.vector.tensor_copy(ks[:], swin[a][:].indirect(lists[a][:]))
+            return ks
+
+        def spread(a, col):
+            sp = bank("spread%d" % a, "b%d" % a, [P, 4, P])
+            for t in range(4):
+                nc.tensor.transpose(sp[:, t, :], col[:, t:t + 1].to_broadcast([P, P]), ident[:])
+            return sp
+
+        def scores(a, qq, kw, ks):
+            res = []
+            tot = sbt("tot%d" % a, [P, 2], F32)
+            for h in range(2):
+                sc = bank("sc%d_%d" % (a, h), "b%d" % (2 + h), [P, SLOTS])
+                cols = slice(h * P, (h + 1) * P)
+                nc.tensor.matmul_mx(out=sc[:], lhsT=qq[0][:, cols].bitcast(FP8X4), lhsT_scale=qq[1][:, cols],
+                                    rhs=kw[:].bitcast((FP4X4, FP8X4)[a]), rhs_scale=ks[:], start=True, stop=True)
+                nmax = sbt("nmax%d_%d" % (a, h), [P, 1], F32)
+                nc.vector.tensor_reduce(out=nmax[:], in_=sc[:], axis=AXIS.X, op=ALU.max, negate=True)
+                p = sbt("p%d_%d" % (a, h), [P, SLOTS], F32)
+                nc.scalar.activation(out=p[:], in_=sc[:], func=ACT.Exp, bias=nmax[:], scale=1.0, accum_out=tot[:, h:h + 1])
+                res.append(p)
+            return res, tot
+
+        def weights(a, pt, sp, tag=None):
+            ps_, tot = pt
+            rinv = sbt("rinv%d" % a, [P, 2], F32, tag)
+            nc.vector.reciprocal(out=rinv[:], in_=tot[:])
+            tw = bank("tw%d" % a, "b4", [P, 2, 2, P])
+            for h in range(2):
+                w = sbt("w%d_%d" % (a, h), [P, SLOTS], BF16)
+                nc.vector.scalar_tensor_tensor(
+                    out=w[:].rearrange("p (n t) -> p n t", t=4), in0=ps_[h][:].rearrange("p (n t) -> p n t", t=4),
+                    scalar=rinv[:, h:h + 1], in1=sp[:].rearrange("p t n -> p n t"), op0=ALU.mult, op1=ALU.mult)
+                words = w[:].bitcast(F32)
+                for u in range(2):
+                    nc.tensor.transpose(tw[:, h, u, :], words[:, u::2], ident[:])
+            wt = sbt("wt%d" % a, [P, 4 * ROWS], BF16)
+            nc.scalar.copy(out=wt[:].bitcast(F32).rearrange("p (h q u) -> p h q u", h=2, u=2),
+                           in_=tw[:].rearrange("p h u q -> p h q u"))
+            return wt
+
+        def gather_vals(a, b, on_scalar=False):
+            g = sbt("g%d_%d" % (a, b), [P, SLOTS], BF16)
+            if on_scalar:
+                vb = sbt("vb%d_%d" % (a, b), [P, POOL], BF16)
+                nc.scalar.activation(out=vb[:], in_=vwin[a][b][:], func=ACT.Copy)
+                nc.scalar.activation(out=g[:], in_=vb[:].indirect(lists[a][:]), func=ACT.Copy)
+            else:
+                nc.vector.tensor_copy(g[:], vwin[a][b][:].indirect(lists[a][:]))
+            return g
+
+        def turn(name, gs, dst, tag):
+            n = len(gs)
+            tv = bank(name, tag, [P, n, 2, P])
+            for i, g in enumerate(gs):
+                words = g[:].bitcast(F32)
+                for u in range(2):
+                    nc.tensor.transpose(tv[:, i, u, :], words[:, u::2], ident[:])
+            nc.scalar.copy(out=dst.bitcast(F32).rearrange("p (i e u) -> p i e u", i=n, u=2), in_=tv[:].rearrange("p i u e -> p i e u"))
+
+        def product(dst, vv, b, ww, start, stop):
+            cols = slice(b * P, (b + 1) * P)
+            nc.tensor.matmul_mx(out=dst, lhsT=vv[0][:, cols].bitcast(FP8X4), lhsT_scale=vv[1][:, cols],
+                                rhs=ww[0][:].bitcast(FP8X4), rhs_scale=ww[1][:], start=start, stop=stop)
+
+        def gate_half(j, gg, xx):
+            z = bank("z%d" % j, "b%d" % (2 + j), [P, 2, ROWS])
+            for i in range(2):
+                product(z[:, i, :], gg, i, xx, True, True)
+            th = sbt("th%d" % j, [P, 2, ROWS], F32)
+            nc.scalar.activation(out=th[:], in_=z[:], func=ACT.Tanh, scale=0.5)
+            return th
+
+        def mix(b, th, o, tag=None):
+            t = sbt("t%d" % b, [P, ROWS], F32, tag)
+            nc.vector.scalar_tensor_tensor(out=t[:], in0=th, scalar=-1.0, in1=o[:, 1, :], op0=ALU.add, op1=ALU.mult)
+            return t
+
+        def finish(b, t, o):
+            y = sbt("y%d" % b, [P, ROWS], F32)
+            nc.vector.scalar_tensor_tensor(out=y[:], in0=t[:], scalar=0.5, in1=o[:, 0, :], op0=ALU.mult, op1=ALU.add)
+            nc.sync.dma_start(out=out[b * P:(b + 1) * P, :], in_=y[:])
+
+        def load_words(a):
+            src = keys_words[0] if a == 0 else ikey_words[0].rearrange("p n t -> p (n t)")
+            nc.sync.dma_start(out=kwin[a][:].bitcast(I32), in_=src.bitcast(I32))
+
+        def load_col(a):
+            nc.sync.dma_start(out=wcol[a][:], in_=(size, isz)[a].rearrange("o (p t) -> (o p) t", t=4))
+
+        nc.vector.memset(swin[0][:].bitcast(I32), 0)
+        nc.gpsimd.memset(swin[1][:].bitcast(I32), 0)
+        make_identity(nc, ident[:])
+        nc.sync.dma_start(lists[0][:], offs)
+        load_words(0)
+        load_vals(0, 0)
+        load_scales(0, keys_scales, range(4))
+        nc.sync.dma_start(lists[1][:], offs2)
+        load_col(0)
+        load_rows(qraw[0], query)
+        load_vals(0, 1)
+        load_scales(1, ikey_scales, range(4))
+        load_words(1)
+        load_col(1)
+        load_rows(qraw[1], query2)
+        load_vals(0, 2)
+        load_rows(inraw, inp)
+        load_vals(1, 0)
+        load_vals(0, 3)
+        load_rows(wgraw, wg)
+        load_vals(1, 1)
+        load_vals(1, 2)
+        load_vals(1, 3)
+
+        wneg = sbt("wneg", [P, 4], F32)
+        nc.gpsimd.tensor_scalar(out=wneg[:], in0=wcol[1][:], scalar1=-1.0, scalar2=0.0, op0=ALU.mult, op1=ALU.add)
+
+        kw0 = gather_words(0)
+        ks0 = gather_scales(0)
+        g00 = gather_vals(0, 0, True)
+        qq0 = quantise("q0", weave("q0", qraw[0][:], ROWS, True), ROWS)
+        sp0 = spread(0, wcol[0])
+        pt0 = scores(0, qq0, kw0, ks0)
+        ks1 = gather_scales(1)
+        g01 = gather_vals(0, 1, True)
+        kw1 = gather_words(1)
+        q1b = weave("q1", qraw[1][:], ROWS, True)
+        qq1 = quantise("q1", q1b, ROWS)
+        wt0 = weights(0, pt0, sp0)
+        sp1 = spread(1, wneg)
+        pt1 = scores(1, qq1, kw1, ks1)
+        vta = sbt("vta", [P, 2 * SLOTS], BF16)
+        turn("tv0a", [g00, g01], vta[:], "b5")
+        g02 = gather_vals(0, 2)
+        ww0 = quantise("wt0", wt0, ROWS)
+        vva = quantise("vta", vta, ROWS)
+        acc = []
+
+        def text_products(vv, tags):
+            for i in range(2):
+                o = bank("o%d" % len(acc), tags[i], [P, 2, ROWS])
+                product(o[:, 0, :], vv, i, ww0, True, True)
+                product(o[:, 1, :], vv, i, ww0, True, False)
+                acc.append(o)
+
+        text_products(vva, ("b0", "b5"))
+        wt1 = weights(1, pt1, sp1)
+        xb = weave("x", inraw[:], ROWS)
+        g03 = gather_vals(0, 3)
+        vtb = sbt("vtb", [P, 2 * SLOTS], BF16)
+        turn("tv0b", [g02, g03], vtb[:], "b6")
+        xx = quantise("x", xb, ROWS)
+        ww1 = quantise("wt1", wt1, ROWS)
+        text_products(quantise("vtb", vtb, ROWS), ("b1", "b6"))
+        gi = [gather_vals(1, 0, True)]
+        gate = []
+        for j in range(2):
+            gb = weave("wg%d" % j, wgraw[:, :, j * ROWS:(j + 1) * ROWS], ROWS)
+            gate.append(gate_half(j, quantise("wg%d" % j, gb, ROWS), xx))
+        gi += [gather_vals(1, 1), gather_vals(1, 2), gather_vals(1, 3)]
+        for b in range(4):
+            vt = sbt("vt1_%d" % b, [P, SLOTS], BF16)
+            turn("tv1_%d" % b, [gi[b]], vt[:], ("b7", "b4", "b7", "b4")[b])
+            uu = quantise("vt1_%d" % b, vt, P)
+            product(acc[b][:, 1, :], uu, 0, ww1, False, True)
+            finish(b, mix(b, gate[b // 2][:, b % 2, :], acc[b]), acc[b])

@@ -48,7 +48,9 @@ def tile_attend_fusegate_kernel(tc, query, query2, keys_words, keys_scales, ikey
 
         def load_scales(a, src, quads):
             for q in quads:
-                nc.sync.dma_start(out=swin[a][32 * q:32 * q + 4, :].bitcast(I32), in_=src[0, 4 * q:4 * q + 4, :].bitcast(I32))
+                rows = src[0, 4 * q:4 * q + 4, :].bitcast(I32)
+                nc.sync.dma_start(out=swin[a][32 * q:32 * q + 32, :].bitcast(I32),
+                                  in_=rows.unsqueeze(0).broadcast_to([8, 4, POOL // 4]))
 
         def load_rows(dst, src):
             nc.sync.dma_start(out=dst[:], in_=src.rearrange("(p t) w -> p t w", t=4))
@@ -57,21 +59,22 @@ def tile_attend_fusegate_kernel(tc, query, query2, keys_words, keys_scales, ikey
             nc.sync.dma_start(out=vwin[a][b][:], in_=(vals, ival)[a][b * P:(b + 1) * P, :])
 
 
-        def quantise(name, src, width, tag=None):
-            codes = sbt(name + "_c", [P, width], U32, tag)
-            scales = sbt(name + "_s", [P, width], U8)
-            nc.vector.quantize_mx(out=codes[:].bitcast(FP8X4), scales=scales[:], in_=src[:])
+        def quantise(src, codes, scales):
+            nc.vector.quantize_mx(out=codes.bitcast(FP8X4), scales=scales, in_=src)
             return codes, scales
 
-        def weave(name, raw, width, on_vector=False, tag=None):
-            woven = sbt(name + "_b", [P, 4 * width], BF16, tag)
+        def planes(name, width, tag=None):
+            return sbt(name + "_c", [P, width], U32, tag)[:], sbt(name + "_s", [P, width], U8)[:]
+
+        def weave(name, raw, on_vector=False):
+            woven = sbt(name + "_b", [P, 4 * ROWS], BF16)
             dst = woven[:].rearrange("p (c i t) -> p c t i", i=4, t=4)
             src = raw.rearrange("p t (c i) -> p c t i", i=4)
             if on_vector:
                 nc.vector.tensor_copy(out=dst, in_=src)
             else:
                 nc.scalar.activation(out=dst, in_=src, func=ACT.Copy)
-            return woven
+            return woven[:]
 
         def gather_words(a):
             kw = sbt("kw%d" % a, [P, SLOTS], (U16, U32)[a])
@@ -89,45 +92,15 @@ def tile_attend_fusegate_kernel(tc, query, query2, keys_words, keys_scales, ikey
                 nc.tensor.transpose(sp[:, t, :], col[:, t:t + 1].to_broadcast([P, P]), ident[:])
             return sp
 
-        def scores(a, qq, kw, ks):
-            res = []
-            tot = sbt("tot%d" % a, [P, 2], F32)
-            for h in range(2):
-                sc = bank("sc%d_%d" % (a, h), "b%d" % (2 + h), [P, SLOTS])
-                cols = slice(h * P, (h + 1) * P)
-                nc.tensor.matmul_mx(out=sc[:], lhsT=qq[0][:, cols].bitcast(FP8X4), lhsT_scale=qq[1][:, cols],
-                                    rhs=kw[:].bitcast((FP4X4, FP8X4)[a]), rhs_scale=ks[:], start=True, stop=True)
-                nmax = sbt("nmax%d_%d" % (a, h), [P, 1], F32)
-                nc.vector.tensor_reduce(out=nmax[:], in_=sc[:], axis=AXIS.X, op=ALU.max, negate=True)
-                p = sbt("p%d_%d" % (a, h), [P, SLOTS], F32)
-                nc.scalar.activation(out=p[:], in_=sc[:], func=ACT.Exp, bias=nmax[:], scale=1.0, accum_out=tot[:, h:h + 1])
-                res.append(p)
-            return res, tot
+        def narrow(a, b):
+            vb = sbt("vb%d_%d" % (a, b), [P, POOL], BF16)
+            nc.scalar.activation(out=vb[:], in_=vwin[a][b][:], func=ACT.Copy)
+            return vb
 
-        def weights(a, pt, sp, tag=None):
-            ps_, tot = pt
-            rinv = sbt("rinv%d" % a, [P, 2], F32, tag)
-            nc.vector.reciprocal(out=rinv[:], in_=tot[:])
-            tw = bank("tw%d" % a, "b4", [P, 2, 2, P])
-            for h in range(2):
-                w = sbt("w%d_%d" % (a, h), [P, SLOTS], BF16)
-                nc.vector.scalar_tensor_tensor(
-                    out=w[:].rearrange("p (n t) -> p n t", t=4), in0=ps_[h][:].rearrange("p (n t) -> p n t", t=4),
-                    scalar=rinv[:, h:h + 1], in1=sp[:].rearrange("p t n -> p n t"), op0=ALU.mult, op1=ALU.mult)
-                words = w[:].bitcast(F32)
-                for u in range(2):
-                    nc.tensor.transpose(tw[:, h, u, :], words[:, u::2], ident[:])
-            wt = sbt("wt%d" % a, [P, 4 * ROWS], BF16)
-            nc.scalar.copy(out=wt[:].bitcast(F32).rearrange("p (h q u) -> p h q u", h=2, u=2),
-                           in_=tw[:].rearrange("p h u q -> p h q u"))
-            return wt
-
-        def gather_vals(a, b, on_scalar=False):
+        def gather_vals(a, b, narrowed=None):
             g = sbt("g%d_%d" % (a, b), [P, SLOTS], BF16)
-            if on_scalar:
-                vb = sbt("vb%d_%d" % (a, b), [P, POOL], BF16)
-                nc.scalar.activation(out=vb[:], in_=vwin[a][b][:], func=ACT.Copy)
-                nc.scalar.activation(out=g[:], in_=vb[:].indirect(lists[a][:]), func=ACT.Copy)
+            if narrowed is not None:
+                nc.scalar.activation(out=g[:], in_=narrowed[:].indirect(lists[a][:]), func=ACT.Copy)
             else:
                 nc.vector.tensor_copy(g[:], vwin[a][b][:].indirect(lists[a][:]))
             return g
@@ -141,28 +114,10 @@ def tile_attend_fusegate_kernel(tc, query, query2, keys_words, keys_scales, ikey
                     nc.tensor.transpose(tv[:, i, u, :], words[:, u::2], ident[:])
             nc.scalar.copy(out=dst.bitcast(F32).rearrange("p (i e u) -> p i e u", i=n, u=2), in_=tv[:].rearrange("p i u e -> p i e u"))
 
-        def product(dst, vv, b, ww, start, stop):
+        def product(dst, vv, b, ww, start, stop, dtype=FP8X4):
             cols = slice(b * P, (b + 1) * P)
             nc.tensor.matmul_mx(out=dst, lhsT=vv[0][:, cols].bitcast(FP8X4), lhsT_scale=vv[1][:, cols],
-                                rhs=ww[0][:].bitcast(FP8X4), rhs_scale=ww[1][:], start=start, stop=stop)
-
-        def gate_half(j, gg, xx):
-            z = bank("z%d" % j, "b%d" % (2 + j), [P, 2, ROWS])
-            for i in range(2):
-                product(z[:, i, :], gg, i, xx, True, True)
-            th = sbt("th%d" % j, [P, 2, ROWS], F32)
-            nc.scalar.activation(out=th[:], in_=z[:], func=ACT.Tanh, scale=0.5)
-            return th
-
-        def mix(b, th, o, tag=None):
-            t = sbt("t%d" % b, [P, ROWS], F32, tag)
-            nc.vector.scalar_tensor_tensor(out=t[:], in0=th, scalar=-1.0, in1=o[:, 1, :], op0=ALU.add, op1=ALU.mult)
-            return t
-
-        def finish(b, t, o):
-            y = sbt("y%d" % b, [P, ROWS], F32)
-            nc.vector.scalar_tensor_tensor(out=y[:], in0=t[:], scalar=0.5, in1=o[:, 0, :], op0=ALU.mult, op1=ALU.add)
-            nc.sync.dma_start(out=out[b * P:(b + 1) * P, :], in_=y[:])
+                                rhs=ww[0][:].bitcast(dtype), rhs_scale=ww[1][:], start=start, stop=stop)
 
         def load_words(a):
             src = keys_words[0] if a == 0 else ikey_words[0].rearrange("p n t -> p (n t)")
@@ -171,26 +126,24 @@ def tile_attend_fusegate_kernel(tc, query, query2, keys_words, keys_scales, ikey
         def load_col(a):
             nc.sync.dma_start(out=wcol[a][:], in_=(size, isz)[a].rearrange("o (p t) -> (o p) t", t=4))
 
-        nc.vector.memset(swin[0][:].bitcast(I32), 0)
-        nc.gpsimd.memset(swin[1][:].bitcast(I32), 0)
         make_identity(nc, ident[:])
         nc.sync.dma_start(lists[0][:], offs)
         load_words(0)
         load_vals(0, 0)
         load_scales(0, keys_scales, range(4))
+        load_words(1)
         nc.sync.dma_start(lists[1][:], offs2)
-        load_col(0)
-        load_rows(qraw[0], query)
         load_vals(0, 1)
         load_scales(1, ikey_scales, range(4))
-        load_words(1)
-        load_col(1)
+        load_rows(qraw[0], query)
         load_rows(qraw[1], query2)
-        load_vals(0, 2)
         load_rows(inraw, inp)
-        load_vals(1, 0)
-        load_vals(0, 3)
+        load_col(0)
+        load_col(1)
+        load_vals(0, 2)
         load_rows(wgraw, wg)
+        load_vals(0, 3)
+        load_vals(1, 0)
         load_vals(1, 1)
         load_vals(1, 2)
         load_vals(1, 3)
@@ -198,52 +151,85 @@ def tile_attend_fusegate_kernel(tc, query, query2, keys_words, keys_scales, ikey
         wneg = sbt("wneg", [P, 4], F32)
         nc.gpsimd.tensor_scalar(out=wneg[:], in0=wcol[1][:], scalar1=-1.0, scalar2=0.0, op0=ALU.mult, op1=ALU.add)
 
-        kw0 = gather_words(0)
-        ks0 = gather_scales(0)
-        g00 = gather_vals(0, 0, True)
-        qq0 = quantise("q0", weave("q0", qraw[0][:], ROWS, True), ROWS)
-        sp0 = spread(0, wcol[0])
-        pt0 = scores(0, qq0, kw0, ks0)
-        ks1 = gather_scales(1)
-        g01 = gather_vals(0, 1, True)
-        kw1 = gather_words(1)
-        q1b = weave("q1", qraw[1][:], ROWS, True)
-        qq1 = quantise("q1", q1b, ROWS)
-        wt0 = weights(0, pt0, sp0)
-        sp1 = spread(1, wneg)
-        pt1 = scores(1, qq1, kw1, ks1)
+        kw = [gather_words(0), None]
+        ks = [gather_scales(0), None]
+        gv = [gather_vals(0, b, narrow(0, b)) for b in range(2)]
+        kw[1] = gather_words(1)
+        ks[1] = gather_scales(1)
+        qq = [quantise(weave("q%d" % a, qraw[a][:], True), *planes("q%d" % a, ROWS)) for a in range(2)]
+        sp = [spread(0, wcol[0]), spread(1, wneg)]
+        xb = weave("x", inraw[:])
+
+        nmax = sbt("nmax", [P, 4], F32, "qraw1")
+        pp = sbt("pp", [P, 4, SLOTS], F32, "inraw")
+        tot = sbt("tot", [P, 4], F32)
+        for n in range(4):
+            a, h = divmod(n, 2)
+            sc = bank("sc%d" % n, "b%d" % (2 + n), [P, SLOTS])
+            product(sc[:], qq[a], h, (kw[a], ks[a]), True, True, (FP4X4, FP8X4)[a])
+            nc.vector.tensor_reduce(out=nmax[:, n:n + 1], in_=sc[:], axis=AXIS.X, op=ALU.max, negate=True)
+            nc.scalar.activation(out=pp[:, n, :], in_=sc[:], func=ACT.Exp, bias=nmax[:, n:n + 1], scale=1.0,
+                                 accum_out=tot[:, n:n + 1])
         vta = sbt("vta", [P, 2 * SLOTS], BF16)
-        turn("tv0a", [g00, g01], vta[:], "b5")
-        g02 = gather_vals(0, 2)
-        ww0 = quantise("wt0", wt0, ROWS)
-        vva = quantise("vta", vta, ROWS)
-        acc = []
+        turn("tva", gv, vta[:], "b2")
+        xx = quantise(xb, *planes("x", ROWS))
+        gv.append(gather_vals(0, 2))
+        gb = [weave("wg%d" % j, wgraw[:, :, j * ROWS:(j + 1) * ROWS]) for j in range(2)]
+        ib = narrow(1, 0)
 
-        def text_products(vv, tags):
-            for i in range(2):
-                o = bank("o%d" % len(acc), tags[i], [P, 2, ROWS])
-                product(o[:, 0, :], vv, i, ww0, True, True)
-                product(o[:, 1, :], vv, i, ww0, True, False)
-                acc.append(o)
-
-        text_products(vva, ("b0", "b5"))
-        wt1 = weights(1, pt1, sp1)
-        xb = weave("x", inraw[:], ROWS)
-        g03 = gather_vals(0, 3)
-        vtb = sbt("vtb", [P, 2 * SLOTS], BF16)
-        turn("tv0b", [g02, g03], vtb[:], "b6")
-        xx = quantise("x", xb, ROWS)
-        ww1 = quantise("wt1", wt1, ROWS)
-        text_products(quantise("vtb", vtb, ROWS), ("b1", "b6"))
-        gi = [gather_vals(1, 0, True)]
-        gate = []
+        rinv = sbt("rinv", [P, 4], F32, "vwin0_2")
+        nc.vector.reciprocal(out=rinv[:], in_=tot[:])
+        late = sbt("late", [P, 5 * SLOTS], F32, "vwin1_0")
+        wt = late[:, 0:2 * SLOTS].bitcast(BF16)
+        for a in range(2):
+            ws = []
+            for h in range(2):
+                n = 2 * a + h
+                w = sbt("w%d" % n, [P, SLOTS], BF16)
+                nc.vector.scalar_tensor_tensor(
+                    out=w[:].rearrange("p (n t) -> p n t", t=4), in0=pp[:, n, :].rearrange("p (n t) -> p n t", t=4),
+                    scalar=rinv[:, n:n + 1], in1=sp[a][:].rearrange("p t n -> p n t"), op0=ALU.mult, op1=ALU.mult)
+                ws.append(w)
+            turn("tw%d" % a, ws, wt[:, a * 2 * SLOTS:(a + 1) * 2 * SLOTS], ("b6", "b3")[a])
+        vva = quantise(vta[:], *planes("vta", ROWS, "g0_2"))
+        gv.append(gather_vals(0, 3))
+        gi = [gather_vals(1, 0, ib)]
+        vtb = late[:, 2 * SLOTS:3 * SLOTS].bitcast(BF16)
+        turn("tvb", gv[2:4], vtb, "b7")
+        gate = late[:, 3 * SLOTS:5 * SLOTS]
         for j in range(2):
-            gb = weave("wg%d" % j, wgraw[:, :, j * ROWS:(j + 1) * ROWS], ROWS)
-            gate.append(gate_half(j, quantise("wg%d" % j, gb, ROWS), xx))
-        gi += [gather_vals(1, 1), gather_vals(1, 2), gather_vals(1, 3)]
+            gg = quantise(gb[j], *planes("wg%d" % j, ROWS))
+            z = bank("z%d" % j, "b%d" % (4 + j), [P, 2, ROWS])
+            for i in range(2):
+                product(z[:, i, :], gg, i, xx, True, True)
+            nc.scalar.activation(out=gate[:, j * SLOTS:(j + 1) * SLOTS], in_=z[:].rearrange("p i q -> p (i q)"),
+                                 func=ACT.Tanh, scale=0.5)
+        gi += [gather_vals(1, b) for b in range(1, 4)]
+        wc, wsc = planes("wv", 3 * ROWS, "vwin1_1")
+        quantise(wt, wc[:, 0:2 * ROWS], wsc[:, 0:2 * ROWS])
+        ww = [(wc[:, a * ROWS:(a + 1) * ROWS], wsc[:, a * ROWS:(a + 1) * ROWS]) for a in range(2)]
+        vvb = quantise(vtb, wc[:, 2 * ROWS:], wsc[:, 2 * ROWS:])
+        vt = [sbt("vt1_%d" % b, [P, SLOTS], BF16) for b in range(4)]
         for b in range(4):
-            vt = sbt("vt1_%d" % b, [P, SLOTS], BF16)
-            turn("tv1_%d" % b, [gi[b]], vt[:], ("b7", "b4", "b7", "b4")[b])
-            uu = quantise("vt1_%d" % b, vt, P)
-            product(acc[b][:, 1, :], uu, 0, ww1, False, True)
-            finish(b, mix(b, gate[b // 2][:, b % 2, :], acc[b]), acc[b])
+            turn("tv1_%d" % b, [gi[b]], vt[b][:], ("b3", "b7", "b4", "b5")[b])
+        acc = []
+        for b in range(4):
+            o = bank("o%d" % b, ("b0", "b1", "b2", "b6")[b], [P, 2, ROWS])
+            product(o[:, 0, :], (vva, vvb)[b // 2], b % 2, ww[0], True, True)
+            product(o[:, 1, :], (vva, vvb)[b // 2], b % 2, ww[0], True, False)
+            acc.append(o)
+        uu = planes("u", 4 * P, "vwin1_3")
+        for b in range(4):
+            cols = slice(b * P, (b + 1) * P)
+            quantise(vt[b][:], uu[0][:, cols], uu[1][:, cols])
+            product(acc[b][:, 1, :], uu, b, ww[1], False, True)
+        ts = []
+        for b in range(4):
+            t = sbt("t%d" % b, [P, ROWS], F32)
+            nc.vector.scalar_tensor_tensor(out=t[:], in0=gate[:, b * ROWS:(b + 1) * ROWS], scalar=-1.0, in1=acc[b][:, 1, :],
+                                           op0=ALU.add, op1=ALU.mult)
+            ts.append(t)
+        for b in range(4):
+            y = sbt("y%d" % b, [P, ROWS], F32)
+            nc.vector.scalar_tensor_tensor(out=y[:], in0=ts[b][:], scalar=0.5, in1=acc[b][:, 0, :], op0=ALU.mult, op1=ALU.add)
+            nc.sync.dma_start(out=out[b * P:(b + 1) * P, :], in_=y[:])

@@ -48,9 +48,7 @@ def tile_attend_fusegate_kernel(tc, query, query2, keys_words, keys_scales, ikey
 
         def load_scales(a, src, quads):
             for q in quads:
-                rows = src[0, 4 * q:4 * q + 4, :].bitcast(I32)
-                nc.sync.dma_start(out=swin[a][32 * q:32 * q + 32, :].bitcast(I32),
-                                  in_=rows.unsqueeze(0).broadcast_to([8, 4, POOL // 4]))
+                nc.sync.dma_start(out=swin[a][32 * q:32 * q + 4, :].bitcast(I32), in_=src[0, 4 * q:4 * q + 4, :].bitcast(I32))
 
         def load_rows(dst, src):
             nc.sync.dma_start(out=dst[:], in_=src.rearrange("(p t) w -> p t w", t=4))
@@ -124,22 +122,25 @@ def tile_attend_fusegate_kernel(tc, query, query2, keys_words, keys_scales, ikey
             nc.sync.dma_start(out=kwin[a][:].bitcast(I32), in_=src.bitcast(I32))
 
         def load_col(a):
-            nc.sync.dma_start(out=wcol[a][:], in_=(size, isz)[a].rearrange("o (p t) -> (o p) t", t=4))
+            with nc.allow_non_contiguous_dma(reason="one slot weight to a partition"):
+                nc.sync.dma_start(out=wcol[a][:], in_=(size, isz)[a][0].rearrange("(t p) -> p t", t=4))
 
+        nc.vector.memset(swin[0][:].bitcast(I32), 0)
+        nc.gpsimd.memset(swin[1][:].bitcast(I32), 0)
         make_identity(nc, ident[:])
         nc.sync.dma_start(lists[0][:], offs)
         load_words(0)
         load_vals(0, 0)
         load_scales(0, keys_scales, range(4))
-        load_words(1)
         nc.sync.dma_start(lists[1][:], offs2)
-        load_vals(0, 1)
-        load_scales(1, ikey_scales, range(4))
-        load_rows(qraw[0], query)
-        load_rows(qraw[1], query2)
-        load_rows(inraw, inp)
+        load_words(1)
         load_col(0)
         load_col(1)
+        load_rows(qraw[0], query)
+        load_vals(0, 1)
+        load_scales(1, ikey_scales, range(4))
+        load_rows(qraw[1], query2)
+        load_rows(inraw, inp)
         load_vals(0, 2)
         load_rows(wgraw, wg)
         load_vals(0, 3)
@@ -187,8 +188,8 @@ def tile_attend_fusegate_kernel(tc, query, query2, keys_words, keys_scales, ikey
                 n = 2 * a + h
                 w = sbt("w%d" % n, [P, SLOTS], BF16)
                 nc.vector.scalar_tensor_tensor(
-                    out=w[:].rearrange("p (n t) -> p n t", t=4), in0=pp[:, n, :].rearrange("p (n t) -> p n t", t=4),
-                    scalar=rinv[:, n:n + 1], in1=sp[a][:].rearrange("p t n -> p n t"), op0=ALU.mult, op1=ALU.mult)
+                    out=w[:], in0=pp[:, n, :],
+                    scalar=rinv[:, n:n + 1], in1=sp[a][:].rearrange("p t n -> p (t n)"), op0=ALU.mult, op1=ALU.mult)
                 ws.append(w)
             turn("tw%d" % a, ws, wt[:, a * 2 * SLOTS:(a + 1) * 2 * SLOTS], ("b6", "b3")[a])
         vva = quantise(vta[:], *planes("vta", ROWS, "g0_2"))

@@ -97,10 +97,11 @@ def tile_attend_fusegate_kernel(tc, query, query2, keys_words, keys_scales, ikey
 
         def gather_vals(a, b, narrowed=None):
             g = sbt("g%d_%d" % (a, b), [P, SLOTS], BF16)
+            dealt = g[:].rearrange("p (u k x) -> p k u x", u=2, x=16)
             if narrowed is not None:
-                nc.scalar.activation(out=g[:], in_=narrowed[:].indirect(lists[a][:]), func=ACT.Copy)
+                nc.scalar.activation(out=dealt, in_=narrowed[:].indirect(lists[a][:]), func=ACT.Copy)
             else:
-                nc.vector.tensor_copy(g[:], vwin[a][b][:].indirect(lists[a][:]))
+                nc.vector.tensor_copy(dealt, vwin[a][b][:].indirect(lists[a][:]))
             return g
 
         def turn(name, gs, dst, tag):
@@ -109,7 +110,7 @@ def tile_attend_fusegate_kernel(tc, query, query2, keys_words, keys_scales, ikey
             for i, g in enumerate(gs):
                 words = g[:].bitcast(F32)
                 for u in range(2):
-                    nc.tensor.transpose(tv[:, i, u, :], words[:, u::2], ident[:])
+                    nc.tensor.transpose(tv[:, i, u, :], words[:, u * P:(u + 1) * P], ident[:])
             nc.scalar.copy(out=dst.bitcast(F32).rearrange("p (i e u) -> p i e u", i=n, u=2), in_=tv[:].rearrange("p i u e -> p i e u"))
 
         def product(dst, vv, b, ww, start, stop, dtype=FP8X4):
@@ -181,17 +182,20 @@ def tile_attend_fusegate_kernel(tc, query, query2, keys_words, keys_scales, ikey
         rinv = sbt("rinv", [P, 4], F32, "vwin0_2")
         nc.vector.reciprocal(out=rinv[:], in_=tot[:])
         late = sbt("late", [P, 5 * SLOTS], F32, "vwin1_0")
-        wt = late[:, 0:2 * SLOTS].bitcast(BF16)
+        wt = [sbt("wt0", [P, 2 * SLOTS], BF16, "wgraw")[:], late[:, SLOTS:2 * SLOTS].bitcast(BF16)]
         for a in range(2):
             ws = []
             for h in range(2):
                 n = 2 * a + h
                 w = sbt("w%d" % n, [P, SLOTS], BF16)
-                nc.vector.scalar_tensor_tensor(
-                    out=w[:], in0=pp[:, n, :],
-                    scalar=rinv[:, n:n + 1], in1=sp[a][:].rearrange("p t n -> p (t n)"), op0=ALU.mult, op1=ALU.mult)
+                for u in range(2):
+                    nc.vector.scalar_tensor_tensor(
+                        out=w[:, u * ROWS:(u + 1) * ROWS].rearrange("p (k x) -> p k x", x=16),
+                        in0=pp[:, n, :].rearrange("p (k u x) -> p k u x", u=2, x=16)[:, :, u, :], scalar=rinv[:, n:n + 1],
+                        in1=sp[a][:].rearrange("p t (k u x) -> p (t k) u x", u=2, x=16)[:, :, u, :],
+                        op0=ALU.mult, op1=ALU.mult)
                 ws.append(w)
-            turn("tw%d" % a, ws, wt[:, a * 2 * SLOTS:(a + 1) * 2 * SLOTS], ("b6", "b3")[a])
+            turn("tw%d" % a, ws, wt[a], ("b6", "b3")[a])
         vva = quantise(vta[:], *planes("vta", ROWS, "g0_2"))
         gv.append(gather_vals(0, 3))
         gi = [gather_vals(1, 0, ib)]
@@ -205,20 +209,25 @@ def tile_attend_fusegate_kernel(tc, query, query2, keys_words, keys_scales, ikey
                 product(z[:, i, :], gg, i, xx, True, True)
             nc.scalar.activation(out=gate[:, j * SLOTS:(j + 1) * SLOTS], in_=z[:].rearrange("p i q -> p (i q)"),
                                  func=ACT.Tanh, scale=0.5)
+        acc = []
+
+        def text_products(vv, tags):
+            for i in range(2):
+                o = bank("o%d" % len(acc), tags[i], [P, 2, ROWS])
+                product(o[:, 0, :], vv, i, ww[0], True, True)
+                product(o[:, 1, :], vv, i, ww[0], True, False)
+                acc.append(o)
+
+        ww = [quantise(wt[0], *planes("wt0", ROWS))]
+        text_products(vva, ("b0", "b1"))
         gi += [gather_vals(1, b) for b in range(1, 4)]
-        wc, wsc = planes("wv", 3 * ROWS, "vwin1_1")
-        quantise(wt, wc[:, 0:2 * ROWS], wsc[:, 0:2 * ROWS])
-        ww = [(wc[:, a * ROWS:(a + 1) * ROWS], wsc[:, a * ROWS:(a + 1) * ROWS]) for a in range(2)]
-        vvb = quantise(vtb, wc[:, 2 * ROWS:], wsc[:, 2 * ROWS:])
+        wc, wsc = planes("wv", 2 * ROWS, "vwin1_1")
+        vvb = quantise(vtb, wc[:, ROWS:], wsc[:, ROWS:])
+        ww.append(quantise(wt[1], wc[:, 0:ROWS], wsc[:, 0:ROWS]))
         vt = [sbt("vt1_%d" % b, [P, SLOTS], BF16) for b in range(4)]
         for b in range(4):
             turn("tv1_%d" % b, [gi[b]], vt[b][:], ("b3", "b7", "b4", "b5")[b])
-        acc = []
-        for b in range(4):
-            o = bank("o%d" % b, ("b0", "b1", "b2", "b6")[b], [P, 2, ROWS])
-            product(o[:, 0, :], (vva, vvb)[b // 2], b % 2, ww[0], True, True)
-            product(o[:, 1, :], (vva, vvb)[b // 2], b % 2, ww[0], True, False)
-            acc.append(o)
+        text_products(vvb, ("b2", "b6"))
         uu = planes("u", 4 * P, "vwin1_3")
         for b in range(4):
             cols = slice(b * P, (b + 1) * P)

@@ -20,6 +20,11 @@ POOL = 1024
 SLOTS = 512
 ROWS = 256
 FEATS = 512
+PACK = 4
+RUN = 16
+NEAR = 4
+TEXT, IMAGE = 0, 1
+PER_COLUMN = 16
 FLOPS = 5 * 2 * 512 * 512 * 256
 
 
@@ -33,29 +38,40 @@ def tile_attend_fusegate_kernel(tc, query, query2, keys_words, keys_scales, ikey
         def sbt(name, shape, dtype, tag=None):
             return sb.tile(shape, dtype, name=name, tag=tag or name, align_bytes=64)
 
-        def bank(name, tag, shape):
-            return ps.tile(shape, F32, name=name, tag=tag)
+        def bank(name, number, shape):
+            return ps.tile(shape, F32, name=name, tag="b%d" % number)
 
-        lists = [sbt("list0", [P, SLOTS // 16], U16), sbt("list1", [P, SLOTS // 16], U16)]
+        lists = [sbt("list0", [P, SLOTS // PER_COLUMN], U16), sbt("list1", [P, SLOTS // PER_COLUMN], U16)]
         kwin = [sbt("kwin0", [P, POOL], U16), sbt("kwin1", [P, POOL], U32)]
         swin = [sbt("swin0", [P, POOL], U8), sbt("swin1", [P, POOL], U8)]
-        qraw = [sbt("qraw%d" % a, [P, 4, ROWS], F32) for a in range(2)]
-        wcol = [sbt("wcol%d" % a, [P, 4], F32) for a in range(2)]
+        qraw = [sbt("qraw%d" % a, [P, PACK, ROWS], F32) for a in range(2)]
+        wcol = [sbt("wcol%d" % a, [P, SLOTS // P], F32) for a in range(2)]
         vwin = [[sbt("vwin%d_%d" % (a, b), [P, POOL], F32) for b in range(4)] for a in range(2)]
-        inraw = sbt("inraw", [P, 4, ROWS], F32)
-        wgraw = sbt("wgraw", [P, 4, FEATS], F32)
+        inraw = sbt("inraw", [P, PACK, ROWS], F32)
+        wgraw = sbt("wgraw", [P, PACK, FEATS], F32)
         ident = sbt("ident", [P, P], F32)
 
-        def load_scales(a, src, quads):
-            for q in quads:
+        def load_list(a):
+            nc.sync.dma_start(lists[a][:], (offs, offs2)[a])
+
+        def load_words(a):
+            src = keys_words[0] if a == TEXT else ikey_words[0].rearrange("p n t -> p (n t)")
+            nc.sync.dma_start(out=kwin[a][:].bitcast(I32), in_=src.bitcast(I32))
+
+        def load_scales(a):
+            src = (keys_scales, ikey_scales)[a]
+            for q in range(4):
                 nc.sync.dma_start(out=swin[a][32 * q:32 * q + 4, :].bitcast(I32), in_=src[0, 4 * q:4 * q + 4, :].bitcast(I32))
 
         def load_rows(dst, src):
-            nc.sync.dma_start(out=dst[:], in_=src.rearrange("(p t) w -> p t w", t=4))
+            nc.sync.dma_start(out=dst[:], in_=src.rearrange("(p t) w -> p t w", t=PACK))
 
         def load_vals(a, b):
             nc.sync.dma_start(out=vwin[a][b][:], in_=(vals, ival)[a][b * P:(b + 1) * P, :])
 
+        def load_slot_weights(a):
+            with nc.allow_non_contiguous_dma(reason="one slot weight to a partition and column"):
+                nc.sync.dma_start(out=wcol[a][:], in_=(size, isz)[a][0].rearrange("(t p) -> p t", t=SLOTS // P))
 
         def quantise(src, codes, scales):
             nc.vector.quantize_mx(out=codes.bitcast(FP8X4), scales=scales, in_=src)
@@ -65,181 +81,179 @@ def tile_attend_fusegate_kernel(tc, query, query2, keys_words, keys_scales, ikey
             return sbt(name + "_c", [P, width], U32, tag)[:], sbt(name + "_s", [P, width], U8)[:]
 
         def weave(name, raw, on_vector=False):
-            woven = sbt(name + "_b", [P, 4 * ROWS], BF16)
-            dst = woven[:].rearrange("p (c i t) -> p c t i", i=4, t=4)
-            src = raw.rearrange("p t (c i) -> p c t i", i=4)
+            woven = sbt(name + "_b", [P, PACK * ROWS], BF16)
+            dst = woven[:].rearrange("p (c m t) -> p c t m", m=NEAR, t=PACK)
+            src = raw.rearrange("p t (c m) -> p c t m", m=NEAR)
             if on_vector:
                 nc.vector.tensor_copy(out=dst, in_=src)
             else:
                 nc.scalar.activation(out=dst, in_=src, func=ACT.Copy)
             return woven[:]
 
+        def weave_aside(name, raw, tag):
+            woven = sbt(name + "_b", [P, PACK * ROWS], BF16, tag)
+            nc.gpsimd.tensor_scalar(out=woven[:].rearrange("p (c t) -> p c t", t=PACK), in0=raw.rearrange("p t c -> p c t"),
+                                    scalar1=1.0, scalar2=0.0, op0=ALU.mult, op1=ALU.add)
+            return woven[:]
+
         def gather_words(a):
-            kw = sbt("kw%d" % a, [P, SLOTS], (U16, U32)[a])
-            nc.vector.tensor_copy(kw[:], kwin[a][:].indirect(lists[a][:]))
-            return kw
+            words = sbt("kw%d" % a, [P, SLOTS], (U16, U32)[a])
+            nc.vector.tensor_copy(words[:], kwin[a][:].indirect(lists[a][:]))
+            return words
 
         def gather_scales(a):
-            ks = sbt("ks%d" % a, [P, SLOTS], U8)
-            nc.vector.tensor_copy(ks[:], swin[a][:].indirect(lists[a][:]))
-            return ks
+            scales = sbt("ks%d" % a, [P, SLOTS], U8)
+            nc.vector.tensor_copy(scales[:], swin[a][:].indirect(lists[a][:]))
+            return scales
 
         def spread(a, col):
-            sp = bank("spread%d" % a, "b%d" % a, [P, 4, P])
-            for t in range(4):
-                nc.tensor.transpose(sp[:, t, :], col[:, t:t + 1].to_broadcast([P, P]), ident[:])
-            return sp
+            row = bank("spread%d" % a, a, [P, SLOTS // P, P])
+            for t in range(SLOTS // P):
+                nc.tensor.transpose(row[:, t, :], col[:, t:t + 1].to_broadcast([P, P]), ident[:])
+            return row
 
         def narrow(a, b):
-            vb = sbt("vb%d_%d" % (a, b), [P, POOL], BF16)
-            nc.scalar.activation(out=vb[:], in_=vwin[a][b][:], func=ACT.Copy)
-            return vb
+            window = sbt("vb%d_%d" % (a, b), [P, POOL], BF16)
+            nc.scalar.activation(out=window[:], in_=vwin[a][b][:], func=ACT.Copy)
+            return window
 
         def gather_vals(a, b, narrowed=None):
-            g = sbt("g%d_%d" % (a, b), [P, SLOTS], BF16)
-            dealt = g[:].rearrange("p (u k x) -> p k u x", u=2, x=16)
+            picked = sbt("g%d_%d" % (a, b), [P, SLOTS], BF16)
+            dealt = picked[:].rearrange("p (u g x) -> p g u x", u=2, x=RUN)
             if narrowed is not None:
                 nc.scalar.activation(out=dealt, in_=narrowed[:].indirect(lists[a][:]), func=ACT.Copy)
             else:
                 nc.vector.tensor_copy(dealt, vwin[a][b][:].indirect(lists[a][:]))
-            return g
+            return picked
 
-        def turn(name, gs, dst, tag):
-            n = len(gs)
-            tv = bank(name, tag, [P, n, 2, P])
-            for i, g in enumerate(gs):
-                words = g[:].bitcast(F32)
+        def turn(name, tiles, dst, number):
+            count = len(tiles)
+            turned = bank(name, number, [P, count, 2, P])
+            for s, tile in enumerate(tiles):
+                pairs = tile[:].bitcast(F32)
                 for u in range(2):
-                    nc.tensor.transpose(tv[:, i, u, :], words[:, u * P:(u + 1) * P], ident[:])
-            nc.scalar.copy(out=dst.bitcast(F32).rearrange("p (i e u) -> p i e u", i=n, u=2), in_=tv[:].rearrange("p i u e -> p i e u"))
+                    nc.tensor.transpose(turned[:, s, u, :], pairs[:, u * P:(u + 1) * P], ident[:])
+            nc.scalar.copy(out=dst.bitcast(F32).rearrange("p (s e u) -> p s e u", s=count, u=2),
+                           in_=turned[:].rearrange("p s u e -> p s e u"))
 
-        def product(dst, vv, b, ww, start, stop, dtype=FP8X4):
-            cols = slice(b * P, (b + 1) * P)
-            nc.tensor.matmul_mx(out=dst, lhsT=vv[0][:, cols].bitcast(FP8X4), lhsT_scale=vv[1][:, cols],
-                                rhs=ww[0][:].bitcast(dtype), rhs_scale=ww[1][:], start=start, stop=stop)
+        def product(dst, held, block, moving, start, stop, moving_dtype=FP8X4):
+            cols = slice(block * P, (block + 1) * P)
+            nc.tensor.matmul_mx(out=dst, lhsT=held[0][:, cols].bitcast(FP8X4), lhsT_scale=held[1][:, cols],
+                                rhs=moving[0][:].bitcast(moving_dtype), rhs_scale=moving[1][:], start=start, stop=stop)
 
-        def load_words(a):
-            src = keys_words[0] if a == 0 else ikey_words[0].rearrange("p n t -> p (n t)")
-            nc.sync.dma_start(out=kwin[a][:].bitcast(I32), in_=src.bitcast(I32))
-
-        def load_col(a):
-            with nc.allow_non_contiguous_dma(reason="one slot weight to a partition"):
-                nc.sync.dma_start(out=wcol[a][:], in_=(size, isz)[a][0].rearrange("(t p) -> p t", t=4))
-
-        nc.vector.memset(swin[0][:].bitcast(I32), 0)
-        nc.gpsimd.memset(swin[1][:].bitcast(I32), 0)
+        nc.vector.memset(swin[TEXT][:].bitcast(I32), 0)
+        nc.gpsimd.memset(swin[IMAGE][:].bitcast(I32), 0)
         make_identity(nc, ident[:])
-        nc.sync.dma_start(lists[0][:], offs)
-        load_words(0)
-        load_vals(0, 0)
-        load_scales(0, keys_scales, range(4))
-        nc.sync.dma_start(lists[1][:], offs2)
-        load_words(1)
-        load_col(0)
-        load_col(1)
-        load_rows(qraw[0], query)
-        load_vals(0, 1)
-        load_scales(1, ikey_scales, range(4))
-        load_rows(qraw[1], query2)
+
+        load_list(TEXT)
+        load_words(TEXT)
+        load_list(IMAGE)
+        load_words(IMAGE)
+        load_vals(TEXT, 0)
+        load_scales(TEXT)
+        load_slot_weights(TEXT)
+        load_rows(qraw[TEXT], query)
+        load_vals(TEXT, 1)
+        load_scales(IMAGE)
+        load_rows(qraw[IMAGE], query2)
         load_rows(inraw, inp)
-        load_vals(0, 2)
+        load_slot_weights(IMAGE)
+        load_vals(TEXT, 2)
         load_rows(wgraw, wg)
-        load_vals(0, 3)
-        load_vals(1, 0)
-        load_vals(1, 1)
-        load_vals(1, 2)
-        load_vals(1, 3)
-
-        wneg = sbt("wneg", [P, 4], F32)
-        nc.gpsimd.tensor_scalar(out=wneg[:], in0=wcol[1][:], scalar1=-1.0, scalar2=0.0, op0=ALU.mult, op1=ALU.add)
-
-        kw = [gather_words(0), None]
-        ks = [gather_scales(0), None]
-        gv = [gather_vals(0, b, narrow(0, b)) for b in range(2)]
-        kw[1] = gather_words(1)
-        ks[1] = gather_scales(1)
-        qq = [quantise(weave("q%d" % a, qraw[a][:], True), *planes("q%d" % a, ROWS)) for a in range(2)]
-        sp = [spread(0, wcol[0]), spread(1, wneg)]
-        xb = weave("x", inraw[:])
-
-        nmax = sbt("nmax", [P, 4], F32, "qraw1")
-        pp = sbt("pp", [P, 4, SLOTS], F32, "inraw")
-        tot = sbt("tot", [P, 4], F32)
-        for n in range(4):
-            a, h = divmod(n, 2)
-            sc = bank("sc%d" % n, "b%d" % (2 + n), [P, SLOTS])
-            product(sc[:], qq[a], h, (kw[a], ks[a]), True, True, (FP4X4, FP8X4)[a])
-            nc.vector.tensor_reduce(out=nmax[:, n:n + 1], in_=sc[:], axis=AXIS.X, op=ALU.max, negate=True)
-            nc.scalar.activation(out=pp[:, n, :], in_=sc[:], func=ACT.Exp, bias=nmax[:, n:n + 1], scale=1.0,
-                                 accum_out=tot[:, n:n + 1])
-        vta = sbt("vta", [P, 2 * SLOTS], BF16)
-        turn("tva", gv, vta[:], "b2")
-        xx = quantise(xb, *planes("x", ROWS))
-        gv.append(gather_vals(0, 2))
-        gb = [weave("wg%d" % j, wgraw[:, :, j * ROWS:(j + 1) * ROWS]) for j in range(2)]
-        ib = narrow(1, 0)
-
-        rinv = sbt("rinv", [P, 4], F32, "vwin0_2")
-        nc.vector.reciprocal(out=rinv[:], in_=tot[:])
-        late = sbt("late", [P, 5 * SLOTS], F32, "vwin1_0")
-        wt = [sbt("wt0", [P, 2 * SLOTS], BF16, "wgraw")[:], late[:, SLOTS:2 * SLOTS].bitcast(BF16)]
-        for a in range(2):
-            ws = []
-            for h in range(2):
-                n = 2 * a + h
-                w = sbt("w%d" % n, [P, SLOTS], BF16)
-                for u in range(2):
-                    nc.vector.scalar_tensor_tensor(
-                        out=w[:, u * ROWS:(u + 1) * ROWS].rearrange("p (k x) -> p k x", x=16),
-                        in0=pp[:, n, :].rearrange("p (k u x) -> p k u x", u=2, x=16)[:, :, u, :], scalar=rinv[:, n:n + 1],
-                        in1=sp[a][:].rearrange("p t (k u x) -> p (t k) u x", u=2, x=16)[:, :, u, :],
-                        op0=ALU.mult, op1=ALU.mult)
-                ws.append(w)
-            turn("tw%d" % a, ws, wt[a], ("b6", "b3")[a])
-        vva = quantise(vta[:], *planes("vta", ROWS, "g0_2"))
-        gv.append(gather_vals(0, 3))
-        gi = [gather_vals(1, 0, ib)]
-        vtb = late[:, 2 * SLOTS:3 * SLOTS].bitcast(BF16)
-        turn("tvb", gv[2:4], vtb, "b7")
-        gate = late[:, 3 * SLOTS:5 * SLOTS]
-        for j in range(2):
-            gg = quantise(gb[j], *planes("wg%d" % j, ROWS))
-            z = bank("z%d" % j, "b%d" % (4 + j), [P, 2, ROWS])
-            for i in range(2):
-                product(z[:, i, :], gg, i, xx, True, True)
-            nc.scalar.activation(out=gate[:, j * SLOTS:(j + 1) * SLOTS], in_=z[:].rearrange("p i q -> p (i q)"),
-                                 func=ACT.Tanh, scale=0.5)
-        acc = []
-
-        def text_products(vv, tags):
-            for i in range(2):
-                o = bank("o%d" % len(acc), tags[i], [P, 2, ROWS])
-                product(o[:, 0, :], vv, i, ww[0], True, True)
-                product(o[:, 1, :], vv, i, ww[0], True, False)
-                acc.append(o)
-
-        ww = [quantise(wt[0], *planes("wt0", ROWS))]
-        text_products(vva, ("b0", "b1"))
-        gi += [gather_vals(1, b) for b in range(1, 4)]
-        wc, wsc = planes("wv", 2 * ROWS, "vwin1_1")
-        vvb = quantise(vtb, wc[:, ROWS:], wsc[:, ROWS:])
-        ww.append(quantise(wt[1], wc[:, 0:ROWS], wsc[:, 0:ROWS]))
-        vt = [sbt("vt1_%d" % b, [P, SLOTS], BF16) for b in range(4)]
+        load_vals(TEXT, 3)
         for b in range(4):
-            turn("tv1_%d" % b, [gi[b]], vt[b][:], ("b3", "b7", "b4", "b5")[b])
-        text_products(vvb, ("b2", "b6"))
-        uu = planes("u", 4 * P, "vwin1_3")
+            load_vals(IMAGE, b)
+
+        image_col = sbt("wneg", [P, SLOTS // P], F32)
+        nc.gpsimd.tensor_scalar(out=image_col[:], in0=wcol[IMAGE][:], scalar1=-1.0, scalar2=0.0, op0=ALU.mult, op1=ALU.add)
+
+        key_words = [gather_words(a) for a in range(2)]
+        key_scales = [gather_scales(a) for a in range(2)]
+        text_vals = [gather_vals(TEXT, b, narrow(TEXT, b)) for b in range(2)]
+        q_mx = [quantise(weave("q%d" % a, qraw[a][:], True), *planes("q%d" % a, ROWS)) for a in range(2)]
+        slot_row = [spread(TEXT, wcol[TEXT]), spread(IMAGE, image_col)]
+        inp_woven = weave_aside("x", inraw[:], "q1_b")
+
+        neg_max = sbt("nmax", [P, 4], F32, "qraw1")
+        expo = sbt("pp", [P, 4, SLOTS], F32)
+        total = sbt("tot", [P, 4], F32)
+        for n in range(4):
+            a, half = divmod(n, 2)
+            score = bank("sc%d" % n, 2 + n, [P, SLOTS])
+            product(score[:], q_mx[a], half, (key_words[a], key_scales[a]), True, True, (FP4X4, FP8X4)[a])
+            nc.vector.tensor_reduce(out=neg_max[:, n:n + 1], in_=score[:], axis=AXIS.X, op=ALU.max, negate=True)
+            nc.scalar.activation(out=expo[:, n, :], in_=score[:], func=ACT.Exp, bias=neg_max[:, n:n + 1], scale=1.0,
+                                 accum_out=total[:, n:n + 1])
+        text_lo = sbt("vta", [P, 2 * SLOTS], BF16)
+        turn("tva", text_vals, text_lo[:], 2)
+        inp_mx = quantise(inp_woven, *planes("x", ROWS))
+        text_vals.append(gather_vals(TEXT, 2))
+        wg_woven = [weave("wg%d" % pair, wgraw[:, :, pair * ROWS:(pair + 1) * ROWS]) for pair in range(2)]
+        image_window = narrow(IMAGE, 0)
+
+        inverse = sbt("rinv", [P, 4], F32, "vwin0_2")
+        nc.vector.reciprocal(out=inverse[:], in_=total[:])
+        late = sbt("late", [P, 5 * SLOTS], F32, "vwin1_0")
+        weights_t = [late[:, a * SLOTS:(a + 1) * SLOTS].bitcast(BF16) for a in range(2)]
+        text_hi = late[:, 2 * SLOTS:3 * SLOTS].bitcast(BF16)
+        gate = late[:, 3 * SLOTS:5 * SLOTS]
+        weights = [sbt("w%d" % n, [P, SLOTS], BF16) for n in range(4)]
+        for n in range(4):
+            for u in range(2):
+                nc.vector.scalar_tensor_tensor(
+                    out=weights[n][:, u * SLOTS // 2:(u + 1) * SLOTS // 2].rearrange("p (g x) -> p g x", x=RUN),
+                    in0=expo[:, n, :].rearrange("p (g u x) -> p g u x", u=2, x=RUN)[:, :, u, :],
+                    scalar=inverse[:, n:n + 1],
+                    in1=slot_row[n // 2][:].rearrange("p t (g u x) -> p (t g) u x", u=2, x=RUN)[:, :, u, :],
+                    op0=ALU.mult, op1=ALU.mult)
+        turn("tw0", weights[0:2], weights_t[TEXT], 6)
+        image_vals = [gather_vals(IMAGE, 0, image_window)]
+        turn("tw1", weights[2:4], weights_t[IMAGE], 3)
+        text_lo_mx = quantise(text_lo[:], *planes("vta", ROWS, "g0_2"))
+        text_vals.append(gather_vals(TEXT, 3))
+        turn("tvb", text_vals[2:4], text_hi, 7)
+
+        for pair in range(2):
+            wg_mx = quantise(wg_woven[pair], *planes("wg%d" % pair, ROWS))
+            z = bank("z%d" % pair, 4 + pair, [P, 2, ROWS])
+            for side in range(2):
+                product(z[:, side, :], wg_mx, side, inp_mx, True, True)
+            nc.scalar.activation(out=gate[:, pair * 2 * ROWS:(pair + 1) * 2 * ROWS], in_=z[:].rearrange("p s q -> p (s q)"),
+                                 func=ACT.Tanh, scale=0.5)
+
+        sums = []
+
+        def text_products(values_mx, numbers):
+            for side in range(2):
+                both = bank("o%d" % len(sums), numbers[side], [P, 2, ROWS])
+                product(both[:, 0, :], values_mx, side, weights_mx[TEXT], True, True)
+                product(both[:, 1, :], values_mx, side, weights_mx[TEXT], True, False)
+                sums.append(both)
+
+        weights_mx = [quantise(weights_t[TEXT], *planes("wt0", ROWS))]
+        text_products(text_lo_mx, (0, 1))
+        image_vals += [gather_vals(IMAGE, b) for b in range(1, 4)]
+        codes, scales = planes("wv", 2 * ROWS, "vwin1_1")
+        text_hi_mx = quantise(text_hi, codes[:, ROWS:], scales[:, ROWS:])
+        weights_mx.append(quantise(weights_t[IMAGE], codes[:, 0:ROWS], scales[:, 0:ROWS]))
+        image_t = [sbt("vt1_%d" % b, [P, SLOTS], BF16) for b in range(4)]
+        for b in range(4):
+            turn("tv1_%d" % b, [image_vals[b]], image_t[b][:], (3, 7, 4, 5)[b])
+        text_products(text_hi_mx, (2, 6))
+        image_mx = planes("u", 4 * P, "vwin1_3")
         for b in range(4):
             cols = slice(b * P, (b + 1) * P)
-            quantise(vt[b][:], uu[0][:, cols], uu[1][:, cols])
-            product(acc[b][:, 1, :], uu, b, ww[1], False, True)
-        ts = []
+            quantise(image_t[b][:], image_mx[0][:, cols], image_mx[1][:, cols])
+            product(sums[b][:, 1, :], image_mx, b, weights_mx[IMAGE], False, True)
+
+        parts = []
         for b in range(4):
-            t = sbt("t%d" % b, [P, ROWS], F32)
-            nc.vector.scalar_tensor_tensor(out=t[:], in0=gate[:, b * ROWS:(b + 1) * ROWS], scalar=-1.0, in1=acc[b][:, 1, :],
-                                           op0=ALU.add, op1=ALU.mult)
-            ts.append(t)
+            part = sbt("t%d" % b, [P, ROWS], F32)
+            nc.vector.scalar_tensor_tensor(out=part[:], in0=gate[:, b * ROWS:(b + 1) * ROWS], scalar=-1.0,
+                                           in1=sums[b][:, 1, :], op0=ALU.add, op1=ALU.mult)
+            parts.append(part)
         for b in range(4):
-            y = sbt("y%d" % b, [P, ROWS], F32)
-            nc.vector.scalar_tensor_tensor(out=y[:], in0=ts[b][:], scalar=0.5, in1=acc[b][:, 0, :], op0=ALU.mult, op1=ALU.add)
-            nc.sync.dma_start(out=out[b * P:(b + 1) * P, :], in_=y[:])
+            mixed = sbt("y%d" % b, [P, ROWS], F32)
+            nc.vector.scalar_tensor_tensor(out=mixed[:], in0=parts[b][:], scalar=0.5, in1=sums[b][:, 0, :],
+                                           op0=ALU.mult, op1=ALU.add)
+            nc.sync.dma_start(out=out[b * P:(b + 1) * P, :], in_=mixed[:])

from contextlib import ExitStack

import concourse.mybir as mybir
from concourse.masks import make_identity

F32 = mybir.dt.float32
BF16 = mybir.dt.bfloat16
I32 = mybir.dt.int32
U32 = mybir.dt.uint32
U16 = mybir.dt.uint16
U8 = mybir.dt.uint8
FP8X4 = mybir.dt.float8_e4m3fn_x4
FP4X4 = mybir.dt.float4_e2m1fn_x4
ALU = mybir.AluOpType
ACT = mybir.ActivationFunctionType
AXIS = mybir.AxisListType

P = 128
POOL = 1024
SLOTS = 512
ROWS = 256
FEATS = 512
PACK = 4
RUN = 16
NEAR = 4
TEXT, IMAGE = 0, 1
PER_COLUMN = 16
FLOPS = 5 * 2 * 512 * 512 * 256


def tile_attend_fusegate_kernel(tc, query, query2, keys_words, keys_scales, ikey_words, ikey_scales,
                                 size, isz, vals, ival, inp, wg, offs, offs2, out):
    nc = tc.nc
    with ExitStack() as ctx:
        sb = ctx.enter_context(tc.tile_pool(name="sb", bufs=1))
        ps = ctx.enter_context(tc.psum_pool(name="ps", bufs=1))

        def sbt(name, shape, dtype, tag=None):
            return sb.tile(shape, dtype, name=name, tag=tag or name, align_bytes=64)

        def bank(name, number, shape):
            return ps.tile(shape, F32, name=name, tag="b%d" % number)

        lists = [sbt("list0", [P, SLOTS // PER_COLUMN], U16), sbt("list1", [P, SLOTS // PER_COLUMN], U16)]
        kwin = [sbt("kwin0", [P, POOL], U16), sbt("kwin1", [P, POOL], U32)]
        swin = [sbt("swin0", [P, POOL], U8), sbt("swin1", [P, POOL], U8)]
        qraw = [sbt("qraw%d" % a, [P, PACK, ROWS], F32) for a in range(2)]
        wcol = [sbt("wcol%d" % a, [P, SLOTS // P], F32) for a in range(2)]
        vwin = [[sbt("vwin%d_%d" % (a, b), [P, POOL], F32) for b in range(4)] for a in range(2)]
        inraw = sbt("inraw", [P, PACK, ROWS], F32)
        wgraw = sbt("wgraw", [P, PACK, FEATS], F32)
        ident = sbt("ident", [P, P], F32)

        def load_list(a):
            nc.sync.dma_start(lists[a][:], (offs, offs2)[a])

        def load_words(a):
            src = keys_words[0] if a == TEXT else ikey_words[0].rearrange("p n t -> p (n t)")
            nc.sync.dma_start(out=kwin[a][:].bitcast(I32), in_=src.bitcast(I32))

        def load_scales(a):
            src = (keys_scales, ikey_scales)[a]
            for q in range(4):
                nc.sync.dma_start(out=swin[a][32 * q:32 * q + 4, :].bitcast(I32), in_=src[0, 4 * q:4 * q + 4, :].bitcast(I32))

        def load_rows(dst, src):
            nc.sync.dma_start(out=dst[:], in_=src.rearrange("(p t) w -> p t w", t=PACK))

        def load_vals(a, b):
            nc.sync.dma_start(out=vwin[a][b][:], in_=(vals, ival)[a][b * P:(b + 1) * P, :])

        def load_slot_weights(a):
            with nc.allow_non_contiguous_dma(reason="one slot weight to a partition and column"):
                nc.sync.dma_start(out=wcol[a][:], in_=(size, isz)[a][0].rearrange("(t p) -> p t", t=SLOTS // P))

        def quantise(src, codes, scales):
            nc.vector.quantize_mx(out=codes.bitcast(FP8X4), scales=scales, in_=src)
            return codes, scales

        def planes(name, width, tag=None):
            return sbt(name + "_c", [P, width], U32, tag)[:], sbt(name + "_s", [P, width], U8)[:]

        def weave(name, raw, on_vector=False):
            woven = sbt(name + "_b", [P, PACK * ROWS], BF16)
            dst = woven[:].rearrange("p (c m t) -> p c t m", m=NEAR, t=PACK)
            src = raw.rearrange("p t (c m) -> p c t m", m=NEAR)
            if on_vector:
                nc.vector.tensor_copy(out=dst, in_=src)
            else:
                nc.scalar.activation(out=dst, in_=src, func=ACT.Copy)
            return woven[:]

        def weave_aside(name, raw, tag):
            woven = sbt(name + "_b", [P, PACK * ROWS], BF16, tag)
            nc.gpsimd.tensor_scalar(out=woven[:].rearrange("p (c t) -> p c t", t=PACK), in0=raw.rearrange("p t c -> p c t"),
                                    scalar1=1.0, scalar2=0.0, op0=ALU.mult, op1=ALU.add)
            return woven[:]

        def gather_words(a):
            words = sbt("kw%d" % a, [P, SLOTS], (U16, U32)[a])
            nc.vector.tensor_copy(words[:], kwin[a][:].indirect(lists[a][:]))
            return words

        def gather_scales(a):
            scales = sbt("ks%d" % a, [P, SLOTS], U8)
            nc.vector.tensor_copy(scales[:], swin[a][:].indirect(lists[a][:]))
            return scales

        def spread(a, col):
            row = bank("spread%d" % a, a, [P, SLOTS // P, P])
            for t in range(SLOTS // P):
                nc.tensor.transpose(row[:, t, :], col[:, t:t + 1].to_broadcast([P, P]), ident[:])
            return row

        def narrow(a, b):
            window = sbt("vb%d_%d" % (a, b), [P, POOL], BF16)
            nc.scalar.activation(out=window[:], in_=vwin[a][b][:], func=ACT.Copy)
            return window

        def gather_vals(a, b, narrowed=None):
            picked = sbt("g%d_%d" % (a, b), [P, SLOTS], BF16)
            dealt = picked[:].rearrange("p (u g x) -> p g u x", u=2, x=RUN)
            if narrowed is not None:
                nc.scalar.activation(out=dealt, in_=narrowed[:].indirect(lists[a][:]), func=ACT.Copy)
            else:
                nc.vector.tensor_copy(dealt, vwin[a][b][:].indirect(lists[a][:]))
            return picked

        def turn(name, tiles, dst, number):
            count = len(tiles)
            turned = bank(name, number, [P, count, 2, P])
            for s, tile in enumerate(tiles):
                pairs = tile[:].bitcast(F32)
                for u in range(2):
                    nc.tensor.transpose(turned[:, s, u, :], pairs[:, u * P:(u + 1) * P], ident[:])
            nc.scalar.copy(out=dst.bitcast(F32).rearrange("p (s e u) -> p s e u", s=count, u=2),
                           in_=turned[:].rearrange("p s u e -> p s e u"))

        def product(dst, held, block, moving, start, stop, moving_dtype=FP8X4):
            cols = slice(block * P, (block + 1) * P)
            nc.tensor.matmul_mx(out=dst, lhsT=held[0][:, cols].bitcast(FP8X4), lhsT_scale=held[1][:, cols],
                                rhs=moving[0][:].bitcast(moving_dtype), rhs_scale=moving[1][:], start=start, stop=stop)

        nc.vector.memset(swin[TEXT][:].bitcast(I32), 0)
        nc.gpsimd.memset(swin[IMAGE][:].bitcast(I32), 0)
        make_identity(nc, ident[:])

        load_list(TEXT)
        load_words(TEXT)
        load_list(IMAGE)
        load_words(IMAGE)
        load_vals(TEXT, 0)
        load_scales(TEXT)
        load_slot_weights(TEXT)
        load_rows(qraw[TEXT], query)
        load_vals(TEXT, 1)
        load_scales(IMAGE)
        load_rows(qraw[IMAGE], query2)
        load_rows(inraw, inp)
        load_slot_weights(IMAGE)
        load_vals(TEXT, 2)
        load_rows(wgraw, wg)
        load_vals(TEXT, 3)
        for b in range(4):
            load_vals(IMAGE, b)

        image_col = sbt("wneg", [P, SLOTS // P], F32)
        nc.gpsimd.tensor_scalar(out=image_col[:], in0=wcol[IMAGE][:], scalar1=-1.0, scalar2=0.0, op0=ALU.mult, op1=ALU.add)

        key_words = [gather_words(a) for a in range(2)]
        key_scales = [gather_scales(a) for a in range(2)]
        text_vals = [gather_vals(TEXT, b, narrow(TEXT, b)) for b in range(2)]
        q_mx = [quantise(weave("q%d" % a, qraw[a][:], True), *planes("q%d" % a, ROWS)) for a in range(2)]
        slot_row = [spread(TEXT, wcol[TEXT]), spread(IMAGE, image_col)]
        inp_woven = weave_aside("x", inraw[:], "q1_b")

        neg_max = sbt("nmax", [P, 4], F32, "qraw1")
        expo = sbt("pp", [P, 4, SLOTS], F32)
        total = sbt("tot", [P, 4], F32)
        for n in range(4):
            a, half = divmod(n, 2)
            score = bank("sc%d" % n, 2 + n, [P, SLOTS])
            product(score[:], q_mx[a], half, (key_words[a], key_scales[a]), True, True, (FP4X4, FP8X4)[a])
            nc.vector.tensor_reduce(out=neg_max[:, n:n + 1], in_=score[:], axis=AXIS.X, op=ALU.max, negate=True)
            nc.scalar.activation(out=expo[:, n, :], in_=score[:], func=ACT.Exp, bias=neg_max[:, n:n + 1], scale=1.0,
                                 accum_out=total[:, n:n + 1])
        text_lo = sbt("vta", [P, 2 * SLOTS], BF16)
        turn("tva", text_vals, text_lo[:], 2)
        inp_mx = quantise(inp_woven, *planes("x", ROWS))
        text_vals.append(gather_vals(TEXT, 2))
        wg_woven = [weave("wg%d" % pair, wgraw[:, :, pair * ROWS:(pair + 1) * ROWS]) for pair in range(2)]
        image_window = narrow(IMAGE, 0)

        inverse = sbt("rinv", [P, 4], F32, "vwin0_2")
        nc.vector.reciprocal(out=inverse[:], in_=total[:])
        late = sbt("late", [P, 5 * SLOTS], F32, "vwin1_0")
        weights_t = [late[:, a * SLOTS:(a + 1) * SLOTS].bitcast(BF16) for a in range(2)]
        text_hi = late[:, 2 * SLOTS:3 * SLOTS].bitcast(BF16)
        gate = late[:, 3 * SLOTS:5 * SLOTS]
        weights = [sbt("w%d" % n, [P, SLOTS], BF16) for n in range(4)]
        for n in range(4):
            for u in range(2):
                nc.vector.scalar_tensor_tensor(
                    out=weights[n][:, u * SLOTS // 2:(u + 1) * SLOTS // 2].rearrange("p (g x) -> p g x", x=RUN),
                    in0=expo[:, n, :].rearrange("p (g u x) -> p g u x", u=2, x=RUN)[:, :, u, :],
                    scalar=inverse[:, n:n + 1],
                    in1=slot_row[n // 2][:].rearrange("p t (g u x) -> p (t g) u x", u=2, x=RUN)[:, :, u, :],
                    op0=ALU.mult, op1=ALU.mult)
        turn("tw0", weights[0:2], weights_t[TEXT], 6)
        image_vals = [gather_vals(IMAGE, 0, image_window)]
        turn("tw1", weights[2:4], weights_t[IMAGE], 3)
        text_lo_mx = quantise(text_lo[:], *planes("vta", ROWS, "g0_2"))
        text_vals.append(gather_vals(TEXT, 3))
        turn("tvb", text_vals[2:4], text_hi, 7)

        for pair in range(2):
            wg_mx = quantise(wg_woven[pair], *planes("wg%d" % pair, ROWS))
            z = bank("z%d" % pair, 4 + pair, [P, 2, ROWS])
            for side in range(2):
                product(z[:, side, :], wg_mx, side, inp_mx, True, True)
            nc.scalar.activation(out=gate[:, pair * 2 * ROWS:(pair + 1) * 2 * ROWS], in_=z[:].rearrange("p s q -> p (s q)"),
                                 func=ACT.Tanh, scale=0.5)

        sums = []

        def text_products(values_mx, numbers):
            for side in range(2):
                both = bank("o%d" % len(sums), numbers[side], [P, 2, ROWS])
                product(both[:, 0, :], values_mx, side, weights_mx[TEXT], True, True)
                product(both[:, 1, :], values_mx, side, weights_mx[TEXT], True, False)
                sums.append(both)

        weights_mx = [quantise(weights_t[TEXT], *planes("wt0", ROWS))]
        text_products(text_lo_mx, (0, 1))
        image_vals += [gather_vals(IMAGE, b) for b in range(1, 4)]
        codes, scales = planes("wv", 2 * ROWS, "vwin1_1")
        text_hi_mx = quantise(text_hi, codes[:, ROWS:], scales[:, ROWS:])
        weights_mx.append(quantise(weights_t[IMAGE], codes[:, 0:ROWS], scales[:, 0:ROWS]))
        image_t = [sbt("vt1_%d" % b, [P, SLOTS], BF16) for b in range(4)]
        for b in range(4):
            turn("tv1_%d" % b, [image_vals[b]], image_t[b][:], (3, 7, 4, 5)[b])
        text_products(text_hi_mx, (2, 6))
        image_mx = planes("u", 4 * P, "vwin1_3")
        for b in range(4):
            cols = slice(b * P, (b + 1) * P)
            quantise(image_t[b][:], image_mx[0][:, cols], image_mx[1][:, cols])
            product(sums[b][:, 1, :], image_mx, b, weights_mx[IMAGE], False, True)

        parts = []
        for b in range(4):
            part = sbt("t%d" % b, [P, ROWS], F32)
            nc.vector.scalar_tensor_tensor(out=part[:], in0=gate[:, b * ROWS:(b + 1) * ROWS], scalar=-1.0,
                                           in1=sums[b][:, 1, :], op0=ALU.add, op1=ALU.mult)
            parts.append(part)
        for b in range(4):
            mixed = sbt("y%d" % b, [P, ROWS], F32)
            nc.vector.scalar_tensor_tensor(out=mixed[:], in0=parts[b][:], scalar=0.5, in1=sums[b][:, 0, :],
                                           op0=ALU.mult, op1=ALU.add)
            nc.sync.dma_start(out=out[b * P:(b + 1) * P, :], in_=mixed[:])
